import numpy as np
import ml_dtypes


def mxq(x, axis, fmt="e4m3"):
    dtype, down = {"e4m3": (ml_dtypes.float8_e4m3fn, 7), "e5m2": (ml_dtypes.float8_e5m2, 14)}[fmt]
    v = np.moveaxis(np.asarray(x, np.float32).astype(ml_dtypes.bfloat16).astype(np.float64), axis, -1)
    blocks = v.reshape(v.shape[:-1] + (-1, 32))
    amax = np.abs(blocks).max(-1, keepdims=True)
    byte = np.maximum(np.where(amax > 0, np.frexp(amax)[1] - 1 + 127, 0) - down, 1)
    scale = np.exp2(byte - 127.0)
    codes = (blocks / scale).astype(np.float32).astype(dtype).astype(np.float64)
    return np.moveaxis((codes * scale).reshape(v.shape), -1, axis)


WIDE = False


def mx_kscale(k):
    if not WIDE:
        return np.ones(k)
    levels = np.array([10, -10, 5, -5, 0])
    if k % 512:
        return np.exp2(np.random.permutation(np.resize(levels, k // 32))).repeat(32)
    a = np.empty((k // 512, 16))
    for p in range(k // 512):
        a[p, :8] = np.random.permutation(np.resize(levels, 8))
        for g in range(8):
            far = levels[np.abs(levels - a[p, g]) >= 10]
            a[p, g + 8] = far[np.random.randint(len(far))]
    return np.exp2(a.ravel()).repeat(32)


def f64(x):
    return np.asarray(x).astype(np.float64)


def striped(idx):
    return np.tile(idx.reshape(-1, 16).T, (8, 1)).astype(np.uint16)


def unstriped(offs):
    return offs[:16].T.reshape(-1).astype(np.int64)


def striped8(idx):
    return np.concatenate([x.reshape(-1, 16).T for x in idx]).astype(np.uint16)


def runs(offs, k):
    lists = np.stack([offs[16 * r : 16 * r + 16].T.reshape(-1) for r in range(8)]).astype(np.int64)
    return lists[np.arange(k) % 512 // 64]


def pack_weight(w):
    k, n = w.shape
    w = f64(np.asarray(w, np.float32).astype(ml_dtypes.bfloat16)).reshape(k // 32, 32, n)
    amax = np.abs(w).max(1)
    byte = np.clip(np.where(amax > 0, np.frexp(amax)[1] - 1 + 127 - 7, 1), 1, 254)
    scaled = (w * np.exp2(127.0 - byte)[:, None, :]).reshape(k, n).astype(np.float32)
    words = np.ascontiguousarray(scaled.reshape(k // 512, 128, 4, n).transpose(0, 1, 3, 2)).astype(ml_dtypes.float8_e4m3fn).view(np.uint8)
    return words, np.ascontiguousarray(byte.astype(np.uint8).reshape(k // 512, 16, n))


def unpack_weight(words, scales):
    g, p, n, _ = words.shape
    vals = np.ascontiguousarray(words).view(ml_dtypes.float8_e4m3fn).astype(np.float64) * np.repeat(np.exp2(scales.astype(np.float64) - 127.0), 8, axis=1)[..., None]
    return vals.transpose(0, 1, 3, 2).reshape(g * 512, n)

def planes(y):
    n, m = y.shape
    v = y.astype(np.float32).astype(ml_dtypes.bfloat16).astype(np.float64).reshape(n // 32, 32, m)
    top = np.abs(v).max(1)
    byte = np.clip(np.where(top > 0, np.frexp(top)[1] - 1 + 127 - 7, 1), 1, 254)
    codes = (v * np.exp2(127.0 - byte)[:, None, :]).reshape(n, m).astype(np.float32).astype(ml_dtypes.float8_e4m3fn).view(np.uint8)
    words = codes.reshape(n // 512, 128, 4, m).transpose(0, 1, 3, 2)
    return np.ascontiguousarray(words), np.ascontiguousarray(byte.astype(np.uint8).reshape(n // 512, 16, m))


K, T, S, H, C = 512, 2048, 512, 512, 512


def setup_inputs():
    n = np.random.standard_normal
    s = mx_kscale(K)[:, None]
    packed_xT = pack_weight(n((K, T)) * s)
    packed_w1 = pack_weight(n((K, H)) / np.sqrt(K) / s)
    packed_w2 = pack_weight(n((K, H)) / np.sqrt(K) / s)
    return {
        "x_words": packed_xT[0],
        "x_scales": packed_xT[1],
        "w1_words": packed_w1[0],
        "w1_scales": packed_w1[1],
        "w2_words": packed_w2[0],
        "w2_scales": packed_w2[1],
        "gs": (np.random.uniform(0.5, 1.5, (K, 1)) / s).astype(np.float32),
        "offs": striped(np.random.permutation(T)[:S]),
        "two": striped(np.random.permutation(T)[:S]),
        "n1": striped8(np.stack([np.random.permutation(S) for _ in range(8)])),
        "n2": striped8(np.stack([np.random.permutation(S) for _ in range(8)])),
        "n3": striped8(np.stack([np.random.permutation(S) for _ in range(8)])),
        "cand": striped(np.random.permutation(T)[:C]),
        "n4": striped8(np.stack([np.random.permutation(S) for _ in range(8)])),
        "n5": striped8(np.stack([np.random.permutation(S) for _ in range(8)])),
        "n6": striped8(np.stack([np.random.permutation(S) for _ in range(8)])),
    }


def reference(x_words, x_scales, w1_words, w1_scales, w2_words, w2_scales, gs, offs, two, n1, n2, n3, cand, n4, n5, n6):
    x_cand = unpack_weight(x_words, x_scales)[:, unstriped(cand)]
    x_two = unpack_weight(x_words, x_scales)[:, unstriped(two)]
    d = unpack_weight(w2_words, w2_scales).T @ x_two
    xq = unpack_weight(x_words, x_scales)[:, unstriped(offs)]
    y = unpack_weight(w1_words, w1_scales).T @ xq
    z = f64(gs) * (d * (y[np.arange(H)[:, None], runs(n1, H)] - y) + 0.5 * ((d[np.arange(H)[:, None], runs(n3, H)]) * (y[np.arange(H)[:, None], runs(n2, H)] - y)))
    s = 0.0625 * ((x_cand.T @ mxq(z, 0, "e4m3")))
    ex = np.exp(0.5 * s)
    out_0 = np.log((ex + ex[np.arange(C)[:, None], runs(n4, C)]) / (ex[np.arange(C)[:, None], runs(n5, C)] + ex[np.arange(C)[:, None], runs(n6, C)]))
    return (out_0,) + planes(out_0)

@@ -1,0 +1,199 @@
+from contextlib import ExitStack
+
+import concourse.mybir as mybir
+
+K, T, S = 512, 2048, 512
+FLOPS = 3 * 2 * 512 * 512 * 512
+
+F32 = mybir.dt.float32
+BF16 = mybir.dt.bfloat16
+I32 = mybir.dt.int32
+U32 = mybir.dt.uint32
+U16 = mybir.dt.uint16
+U8 = mybir.dt.uint8
+FP8X4 = mybir.dt.float8_e4m3fn_x4
+ACT = mybir.ActivationFunctionType
+ALU = mybir.AluOpType
+
+P = 128
+PACK = 4
+HALF = 256
+HALVES = S // HALF
+
+
+def tile_picked_twcflowbodds_none_po_kernel(
+    tc, x_words, x_scales, w1_words, w1_scales, w2_words, w2_scales, gs,
+    offs, two, n1, n2, n3, cand, n4, n5, n6, out_0, out_1, out_2,
+):
+    nc = tc.nc
+    with ExitStack() as ctx:
+        lists = ctx.enter_context(tc.tile_pool(name="lists", bufs=1))
+        keep = ctx.enter_context(tc.tile_pool(name="keep", bufs=1))
+        psum = ctx.enter_context(tc.psum_pool(name="psum", bufs=1))
+
+        def sb(name, shape, dtype):
+            return keep.tile(shape, dtype, name=name, align_bytes=64)
+
+        def load_list(name, source):
+            tile = lists.tile([P, S // 16], U16, name=name)
+            nc.sync.dma_start(tile[:], source)
+            return tile
+
+        def load_words(name, source, width):
+            tile = sb(name, [P, width], I32)
+            nc.sync.dma_start(tile[:], source[0].rearrange("p n t -> p (n t)").bitcast(I32))
+            return tile
+
+        def load_scales(tile, source, queue):
+            for q in range(4):
+                queue.dma_start(tile[32 * q : 32 * q + 4, :].bitcast(I32), source[0, 4 * q : 4 * q + 4, :].bitcast(I32))
+
+        def deal(name, source, dtype):
+            tile = sb(name, [P, S], dtype)
+            nc.vector.tensor_copy(tile[:].rearrange("p (t m) -> p t m", t=PACK), source.rearrange("p (m t) -> p t m", t=PACK))
+            return tile
+
+        def cols(h):
+            return slice(h * HALF, (h + 1) * HALF)
+
+        def entries(tile, h):
+            return tile[:, h * HALF // 16 : (h + 1) * HALF // 16]
+
+        xs = sb("xs", [P, T], U8)
+        w1s_raw = sb("w1s_raw", [P, S], U8)
+        w2s_raw = sb("w2s_raw", [P, S], U8)
+        nc.vector.memset(xs[:].bitcast(I32), 0)
+        nc.gpsimd.memset(w2s_raw[:].bitcast(I32), 0)
+        nc.gpsimd.memset(w1s_raw[:].bitcast(I32), 0)
+
+        gain = sb("gain", [P, PACK], F32)
+        nc.gpsimd.dma_start(gain[:], gs.rearrange("(p t) o -> p (t o)", t=PACK))
+        w1w_raw = load_words("w1w_raw", w1_words, S)
+        load_scales(xs, x_scales, nc.sync)
+        offs_l = load_list("offs_l", offs)
+        two_l = load_list("two_l", two)
+        xw = load_words("xw", x_words, T)
+        load_scales(w1s_raw, w1_scales, nc.sync)
+        w2w_raw = load_words("w2w_raw", w2_words, S)
+        load_scales(w2s_raw, w2_scales, nc.sync)
+        cand_l = load_list("cand_l", cand)
+        n2_l = load_list("n2_l", n2)
+        n1_l = load_list("n1_l", n1)
+        n3_l = load_list("n3_l", n3)
+        n4_l = load_list("n4_l", n4)
+        n5_l = load_list("n5_l", n5)
+        n6_l = load_list("n6_l", n6)
+
+        half_gain = sb("half_gain", [P, PACK], F32)
+        nc.scalar.activation(half_gain[:], gain[:], ACT.Copy, scale=0.5)
+
+        def pick_bytes(name, offsets):
+            tile = sb(name, [P, S], U8)
+            nc.vector.tensor_copy(tile[:], xs[:].indirect(offsets[:]))
+            return tile
+
+        def pick_words(name, offsets):
+            tile = sb(name, [P, S], U32)
+            nc.vector.tensor_copy(tile[:], xw[:].bitcast(U32).indirect(offsets[:]))
+            return tile
+
+        w1w = deal("w1w", w1w_raw[:], I32)
+        offs_s = pick_bytes("offs_s", offs_l)
+        two_s = pick_bytes("two_s", two_l)
+        offs_w = pick_words("offs_w", offs_l)
+        two_w = pick_words("two_w", two_l)
+        w1s = deal("w1s", w1s_raw[:], U8)
+        w2w = deal("w2w", w2w_raw[:], I32)
+        w2s = deal("w2s", w2s_raw[:], U8)
+
+        def product(bank, lhs_w, lhs_s, t, rhs_w, rhs_s):
+            rows = slice(t * P, (t + 1) * P)
+            nc.tensor.matmul_mx(
+                out=bank, lhsT=lhs_w[:, rows].bitcast(FP8X4), lhsT_scale=lhs_s[:, rows],
+                rhs=rhs_w.bitcast(FP8X4), rhs_scale=rhs_s, start=True, stop=True,
+            )
+
+        y_bank = [psum.tile([P, S], F32, name="y_bank%d" % t, tag="bank%d" % t) for t in range(PACK)]
+        d_bank = [psum.tile([P, S], F32, name="d_bank%d" % t, tag="bank%d" % (PACK + t)) for t in range(PACK)]
+        for t in range(PACK):
+            product(y_bank[t][:], w1w, w1s, t, offs_w[:], offs_s[:])
+        for t in range(PACK):
+            product(d_bank[t][:], w2w, w2s, t, two_w[:], two_s[:])
+
+        y_win = [sb("y_win%d" % t, [P, S], F32) for t in range(PACK)]
+        y_own = [sb("y_own%d" % t, [P, S], F32) for t in range(PACK)]
+        d_win = [sb("d_win%d" % t, [P, S], F32) for t in range(PACK)]
+        for t in range(PACK):
+            nc.scalar.copy(y_win[t][:], y_bank[t][:])
+            nc.scalar.copy(y_own[t][:], y_bank[t][:])
+            nc.scalar.activation(d_win[t][:], d_bank[t][:], ACT.Copy, scale=half_gain[:, t : t + 1])
+
+        cand_s = deal("cand_s", pick_bytes("cand_s_list", cand_l)[:], U8)
+        cand_w = deal("cand_w", pick_words("cand_w_list", cand_l)[:].bitcast(I32), I32)
+
+        ex_win = [sb("ex_win%d" % t, [P, S], F32) for t in range(PACK)]
+        s_win = [sb("s_win%d" % t, [P, S], F32) for t in range(PACK)]
+        ex_own = [[sb("ex_own%d_%d" % (h, t), [P, HALF], F32) for t in range(PACK)] for h in range(HALVES)]
+
+        def interleave(engine_copy, dst, src):
+            engine_copy(dst[:].rearrange("p (c i t) -> p c t i", i=4, t=PACK), src[:].rearrange("p t (c i) -> p c t i", i=4))
+
+        for h in range(HALVES):
+            z = sb("z%d" % h, [P, PACK, HALF], F32)
+            for t in range(PACK):
+                u1 = sb("u1_%d_%d" % (h, t), [P, HALF], F32)
+                u2 = sb("u2_%d_%d" % (h, t), [P, HALF], F32)
+                a = sb("a_%d_%d" % (h, t), [P, HALF], F32)
+                b = sb("b_%d_%d" % (h, t), [P, HALF], F32)
+                nc.vector.tensor_tensor(u2[:], y_win[t][:].indirect(entries(n2_l, h)), y_own[t][:, cols(h)], ALU.subtract)
+                nc.vector.tensor_tensor(u1[:], y_win[t][:].indirect(entries(n1_l, h)), y_own[t][:, cols(h)], ALU.subtract)
+                nc.vector.tensor_tensor(b[:], d_win[t][:].indirect(entries(n3_l, h)), u2[:], ALU.mult)
+                nc.vector.scalar_tensor_tensor(a[:], d_win[t][:, cols(h)], 2.0, u1[:], ALU.mult, ALU.mult)
+                nc.vector.tensor_tensor(z[:, t, :], a[:], b[:], ALU.add)
+            z_bf = sb("z_bf%d" % h, [P, PACK * HALF], BF16)
+            interleave(nc.vector.tensor_copy if h == HALVES - 1 else nc.scalar.copy, z_bf, z)
+            z_w = sb("z_w%d" % h, [P, HALF], U32)
+            z_s = sb("z_s%d" % h, [P, HALF], U8)
+            nc.vector.quantize_mx(out=z_w[:].bitcast(FP8X4), scales=z_s[:], in_=z_bf[:])
+            s_bank = [psum.tile([P, HALF], F32, name="s_bank%d_%d" % (h, t), tag="bank%d" % (PACK * h + t)) for t in range(PACK)]
+            for t in range(PACK):
+                product(s_bank[t][:], cand_w, cand_s, t, z_w[:], z_s[:])
+            for t in range(PACK):
+                nc.scalar.activation(ex_win[t][:, cols(h)], s_bank[t][:], ACT.Exp, scale=0.03125)
+                if h == HALVES - 1:
+                    nc.sync.dma_start(ex_own[h][t][:], ex_win[t][:, cols(h)])
+                else:
+                    nc.scalar.activation(ex_own[h][t][:], s_bank[t][:], ACT.Exp, scale=0.03125)
+            for t in range(PACK):
+                nc.scalar.copy(s_win[t][:, cols(h)], s_bank[t][:])
+
+        ex5 = [[sb("ex5_%d_%d" % (h, t), [P, HALF], F32) for t in range(PACK)] for h in range(HALVES)]
+        for h in range(HALVES):
+            for t in range(PACK):
+                nc.scalar.activation(ex5[h][t][:], s_win[t][:].indirect(entries(n5_l, h)), ACT.Exp, scale=0.03125)
+
+        sums = [[sb("sums%d_%d" % (h, t), [P, 2, HALF], F32) for t in range(PACK)] for h in range(HALVES)]
+        for h in range(HALVES):
+            for t in range(PACK):
+                nc.vector.tensor_tensor(sums[h][t][:, 0, :], ex_win[t][:].indirect(entries(n4_l, h)), ex_own[h][t][:], ALU.add)
+            for t in range(PACK):
+                nc.vector.tensor_tensor(sums[h][t][:, 1, :], ex_win[t][:].indirect(entries(n6_l, h)), ex5[h][t][:], ALU.add)
+
+        out_rows = out_0.rearrange("(p t) j -> p t j", t=PACK)
+        out_words = out_1[0].rearrange("p n t -> p (n t)").bitcast(I32)
+        o_s = sb("o_s", [P, S], U8)
+        for h in range(HALVES):
+            o = sb("o%d" % h, [P, PACK, HALF], F32)
+            for t in range(PACK):
+                logs = sb("logs%d_%d" % (h, t), [P, 2, HALF], F32)
+                nc.scalar.activation(logs[:], sums[h][t][:], ACT.Ln)
+                nc.vector.tensor_tensor(o[:, t, :], logs[:, 0, :], logs[:, 1, :], ALU.subtract)
+                nc.sync.dma_start(out_rows[:, t, cols(h)], o[:, t, :])
+            o_bf = sb("o_bf%d" % h, [P, PACK * HALF], BF16)
+            interleave(nc.vector.tensor_copy, o_bf, o)
+            o_w = sb("o_w%d" % h, [P, HALF], U32)
+            nc.vector.quantize_mx(out=o_w[:].bitcast(FP8X4), scales=o_s[:, cols(h)], in_=o_bf[:])
+            nc.sync.dma_start(out_words[:, cols(h)], o_w[:].bitcast(I32))
+        for q in range(4):
+            queue = nc.scalar if q % 2 == 0 else nc.sync
+            queue.dma_start(out_2[0, 4 * q : 4 * q + 4, :].bitcast(I32), o_s[32 * q : 32 * q + 4, :].bitcast(I32))

@@ -1,6 +1,7 @@
 from contextlib import ExitStack
 
 import concourse.mybir as mybir
+from concourse.masks import make_identity
 
 K, T, S = 512, 2048, 512
 FLOPS = 3 * 2 * 512 * 512 * 512
@@ -19,6 +20,10 @@ P = 128
 PACK = 4
 HALF = 256
 HALVES = S // HALF
+EARLY = 384
+LATE = S - EARLY
+WIDE = 2 * S
+OUT_PIECES = ((0, 256, 4), (256, 256, 2))
 
 
 def tile_picked_twcflowbodds_none_po_kernel(
@@ -31,8 +36,11 @@ def tile_picked_twcflowbodds_none_po_kernel(
         keep = ctx.enter_context(tc.tile_pool(name="keep", bufs=1))
         psum = ctx.enter_context(tc.psum_pool(name="psum", bufs=1))
 
-        def sb(name, shape, dtype):
-            return keep.tile(shape, dtype, name=name, align_bytes=64)
+        def sb(name, shape, dtype, tag=None, bufs=1):
+            return keep.tile(shape, dtype, name=name, tag=tag or name, bufs=bufs, align_bytes=64)
+
+        def bank(name, number, shape):
+            return psum.tile(shape, F32, name=name, tag="bank%d" % number)
 
         def load_list(name, source):
             tile = lists.tile([P, S // 16], U16, name=name)
@@ -44,39 +52,38 @@ def tile_picked_twcflowbodds_none_po_kernel(
             nc.sync.dma_start(tile[:], source[0].rearrange("p n t -> p (n t)").bitcast(I32))
             return tile
 
-        def load_scales(tile, source, queue):
+        def load_scales(tile, source, first, queues):
             for q in range(4):
-                queue.dma_start(tile[32 * q : 32 * q + 4, :].bitcast(I32), source[0, 4 * q : 4 * q + 4, :].bitcast(I32))
+                queues[q % len(queues)].dma_start(tile[32 * q + first : 32 * q + first + 4, :].bitcast(I32), source[0, 4 * q : 4 * q + 4, :].bitcast(I32))
 
-        def deal(name, source, dtype):
-            tile = sb(name, [P, S], dtype)
-            nc.vector.tensor_copy(tile[:].rearrange("p (t m) -> p t m", t=PACK), source.rearrange("p (m t) -> p t m", t=PACK))
+        def deal(engine, name, source, dtype, tag=None):
+            tile = sb(name, [P, S], dtype, tag=tag)
+            run = 16 if dtype == U8 else 4
+            engine.tensor_copy(
+                tile[:].rearrange("p (t c i) -> p c t i", t=PACK, i=run),
+                source.rearrange("p (c i t) -> p c t i", t=PACK, i=run),
+            )
             return tile
 
-        def cols(h):
-            return slice(h * HALF, (h + 1) * HALF)
-
-        def entries(tile, h):
-            return tile[:, h * HALF // 16 : (h + 1) * HALF // 16]
+        def entries(tile, first, width):
+            return tile[:, first // 16 : (first + width) // 16]
 
         xs = sb("xs", [P, T], U8)
-        w1s_raw = sb("w1s_raw", [P, S], U8)
-        w2s_raw = sb("w2s_raw", [P, S], U8)
+        ws_raw = sb("ws_raw", [P, S], U8)
         nc.vector.memset(xs[:].bitcast(I32), 0)
-        nc.gpsimd.memset(w2s_raw[:].bitcast(I32), 0)
-        nc.gpsimd.memset(w1s_raw[:].bitcast(I32), 0)
+        nc.vector.memset(ws_raw[:].bitcast(I32), 0)
 
-        gain = sb("gain", [P, PACK], F32)
-        nc.gpsimd.dma_start(gain[:], gs.rearrange("(p t) o -> p (t o)", t=PACK))
         w1w_raw = load_words("w1w_raw", w1_words, S)
-        load_scales(xs, x_scales, nc.sync)
+        load_scales(xs, x_scales, 0, [nc.sync, nc.scalar])
         offs_l = load_list("offs_l", offs)
         two_l = load_list("two_l", two)
         xw = load_words("xw", x_words, T)
-        load_scales(w1s_raw, w1_scales, nc.sync)
+        load_scales(ws_raw, w1_scales, 0, [nc.sync])
+        load_scales(ws_raw, w2_scales, 4, [nc.sync])
         w2w_raw = load_words("w2w_raw", w2_words, S)
-        load_scales(w2s_raw, w2_scales, nc.sync)
         cand_l = load_list("cand_l", cand)
+        gain = sb("gain", [P, PACK], F32)
+        nc.sync.dma_start(gain[:], gs.rearrange("(p t) o -> p (t o)", t=PACK))
         n2_l = load_list("n2_l", n2)
         n1_l = load_list("n1_l", n1)
         n3_l = load_list("n3_l", n3)
@@ -97,103 +104,158 @@ def tile_picked_twcflowbodds_none_po_kernel(
             nc.vector.tensor_copy(tile[:], xw[:].bitcast(U32).indirect(offsets[:]))
             return tile
 
-        w1w = deal("w1w", w1w_raw[:], I32)
+        w1w = deal(nc.vector, "w1w", w1w_raw[:], I32)
         offs_s = pick_bytes("offs_s", offs_l)
         two_s = pick_bytes("two_s", two_l)
         offs_w = pick_words("offs_w", offs_l)
         two_w = pick_words("two_w", two_l)
-        w1s = deal("w1s", w1s_raw[:], U8)
-        w2w = deal("w2w", w2w_raw[:], I32)
-        w2s = deal("w2s", w2s_raw[:], U8)
+        ws = deal(nc.vector, "ws", ws_raw[:], U8)
+        w2w = deal(nc.vector, "w2w", w2w_raw[:], I32)
+        identity = sb("identity", [P, P], F32)
+        make_identity(nc, identity[:])
 
-        def product(bank, lhs_w, lhs_s, t, rhs_w, rhs_s):
+        def product(result, lhs_w, lhs_s, t, rhs_w, rhs_s):
             rows = slice(t * P, (t + 1) * P)
             nc.tensor.matmul_mx(
-                out=bank, lhsT=lhs_w[:, rows].bitcast(FP8X4), lhsT_scale=lhs_s[:, rows],
+                out=result, lhsT=lhs_w[:, rows].bitcast(FP8X4), lhsT_scale=lhs_s[:, rows],
                 rhs=rhs_w.bitcast(FP8X4), rhs_scale=rhs_s, start=True, stop=True,
             )
 
-        y_bank = [psum.tile([P, S], F32, name="y_bank%d" % t, tag="bank%d" % t) for t in range(PACK)]
-        d_bank = [psum.tile([P, S], F32, name="d_bank%d" % t, tag="bank%d" % (PACK + t)) for t in range(PACK)]
+        y_bank = [bank("y_bank%d" % t, t, [P, S]) for t in range(PACK)]
+        d_bank = [bank("d_bank%d" % t, PACK + t, [P, S]) for t in range(PACK)]
         for t in range(PACK):
-            product(y_bank[t][:], w1w, w1s, t, offs_w[:], offs_s[:])
-        for t in range(PACK):
-            product(d_bank[t][:], w2w, w2s, t, two_w[:], two_s[:])
+            product(y_bank[t][:], w1w, ws[:], t, offs_w[:], offs_s[:])
+            product(d_bank[t][:], w2w, ws[4:P, :], t, two_w[:], two_s[:])
 
-        y_win = [sb("y_win%d" % t, [P, S], F32) for t in range(PACK)]
-        y_own = [sb("y_own%d" % t, [P, S], F32) for t in range(PACK)]
-        d_win = [sb("d_win%d" % t, [P, S], F32) for t in range(PACK)]
-        for t in range(PACK):
-            nc.scalar.copy(y_win[t][:], y_bank[t][:])
-            nc.scalar.copy(y_own[t][:], y_bank[t][:])
-            nc.scalar.activation(d_win[t][:], d_bank[t][:], ACT.Copy, scale=half_gain[:, t : t + 1])
+        y_wide = [sb("y_wide%d" % t, [P, WIDE], F32) for t in range(PACK)]
+        y_slim = [sb("y_slim%d" % t, [P, S], F32) for t in range(PACK)]
+        d_wide = [sb("d_wide%d" % t, [P, WIDE], F32) for t in range(PACK)]
 
-        cand_s = deal("cand_s", pick_bytes("cand_s_list", cand_l)[:], U8)
-        cand_w = deal("cand_w", pick_words("cand_w_list", cand_l)[:].bitcast(I32), I32)
+        for t in range(PACK):
+            nc.scalar.copy(y_wide[t][:, :S], y_bank[t][:])
+            nc.scalar.copy(y_slim[t][:], y_bank[t][:])
+            nc.scalar.activation(d_wide[t][:, :S], d_bank[t][:], ACT.Copy, scale=half_gain[:, t : t + 1])
+
+        cand_s_list = pick_bytes("cand_s_list", cand_l)
+        cand_w_list = pick_words("cand_w_list", cand_l)
 
         ex_win = [sb("ex_win%d" % t, [P, S], F32) for t in range(PACK)]
         s_win = [sb("s_win%d" % t, [P, S], F32) for t in range(PACK)]
         ex_own = [[sb("ex_own%d_%d" % (h, t), [P, HALF], F32) for t in range(PACK)] for h in range(HALVES)]
 
         def interleave(engine_copy, dst, src):
-            engine_copy(dst[:].rearrange("p (c i t) -> p c t i", i=4, t=PACK), src[:].rearrange("p t (c i) -> p c t i", i=4))
+            engine_copy(dst.rearrange("p (c i t) -> p c t i", i=2, t=PACK), src.rearrange("p t (c i) -> p c t i", i=2))
 
-        for h in range(HALVES):
-            z = sb("z%d" % h, [P, PACK, HALF], F32)
-            for t in range(PACK):
-                u1 = sb("u1_%d_%d" % (h, t), [P, HALF], F32)
-                u2 = sb("u2_%d_%d" % (h, t), [P, HALF], F32)
-                a = sb("a_%d_%d" % (h, t), [P, HALF], F32)
-                b = sb("b_%d_%d" % (h, t), [P, HALF], F32)
-                nc.vector.tensor_tensor(u2[:], y_win[t][:].indirect(entries(n2_l, h)), y_own[t][:, cols(h)], ALU.subtract)
-                nc.vector.tensor_tensor(u1[:], y_win[t][:].indirect(entries(n1_l, h)), y_own[t][:, cols(h)], ALU.subtract)
-                nc.vector.tensor_tensor(b[:], d_win[t][:].indirect(entries(n3_l, h)), u2[:], ALU.mult)
-                nc.vector.scalar_tensor_tensor(a[:], d_win[t][:, cols(h)], 2.0, u1[:], ALU.mult, ALU.mult)
-                nc.vector.tensor_tensor(z[:, t, :], a[:], b[:], ALU.add)
-            z_bf = sb("z_bf%d" % h, [P, PACK * HALF], BF16)
-            interleave(nc.vector.tensor_copy if h == HALVES - 1 else nc.scalar.copy, z_bf, z)
-            z_w = sb("z_w%d" % h, [P, HALF], U32)
-            z_s = sb("z_s%d" % h, [P, HALF], U8)
-            nc.vector.quantize_mx(out=z_w[:].bitcast(FP8X4), scales=z_s[:], in_=z_bf[:])
-            s_bank = [psum.tile([P, HALF], F32, name="s_bank%d_%d" % (h, t), tag="bank%d" % (PACK * h + t)) for t in range(PACK)]
-            for t in range(PACK):
-                product(s_bank[t][:], cand_w, cand_s, t, z_w[:], z_s[:])
-            for t in range(PACK):
-                nc.scalar.activation(ex_win[t][:, cols(h)], s_bank[t][:], ACT.Exp, scale=0.03125)
-                if h == HALVES - 1:
-                    nc.sync.dma_start(ex_own[h][t][:], ex_win[t][:, cols(h)])
-                else:
-                    nc.scalar.activation(ex_own[h][t][:], s_bank[t][:], ACT.Exp, scale=0.03125)
-            for t in range(PACK):
-                nc.scalar.copy(s_win[t][:, cols(h)], s_bank[t][:])
+        def two_terms(t, first, width, window, own, diffs, a, b):
+            span = slice(first, first + width)
+            nc.vector.tensor_tensor(diffs[:, 1, :], window[:].indirect(entries(n2_l, first, width)), own[:, span], ALU.subtract)
+            nc.vector.tensor_tensor(diffs[:, 0, :], window[:].indirect(entries(n1_l, first, width)), own[:, span], ALU.subtract)
+            nc.vector.tensor_tensor(b, d_wide[t][:].indirect(entries(n3_l, first, width)), diffs[:, 1, :], ALU.mult)
+            nc.vector.scalar_tensor_tensor(a, d_wide[t][:, span], 2.0, diffs[:, 0, :], ALU.mult, ALU.mult)
+
+        def quantise(name, staged, width):
+            words = sb(name + "_w", [P, width], U32)
+            scales = sb(name + "_s", [P, width], U8)
+            nc.vector.quantize_mx(out=words[:].bitcast(FP8X4), scales=scales[:], in_=staged)
+            return words, scales
+
+        blocks = EARLY // P
+        turned = [bank("turned%d" % k, k, [P, PACK, P]) for k in range(blocks)]
+        pairs = [sb("pairs%d" % k, [P, 2, P, 2], BF16) for k in range(blocks)]
+        for t in range(PACK):
+            diffs = sb("diffs%d" % t, [P, 2, EARLY], F32, tag="diffs", bufs=2)
+            a = sb("a%d" % t, [P, EARLY], F32)
+            b = sb("b%d" % t, [P, EARLY], F32)
+            two_terms(t, 0, EARLY, y_wide[t], y_slim[t], diffs, a[:], b[:])
+            for k in range(blocks):
+                part = slice(k * P, (k + 1) * P)
+                nc.tensor.matmul(turned[k][:, t, :], b[:, part], identity[:], start=True, stop=False, is_transpose=True)
+                nc.tensor.matmul(turned[k][:, t, :], a[:, part], identity[:], start=False, stop=True, is_transpose=True)
+            if t % 2 == 1:
+                for k in range(blocks):
+                    nc.scalar.copy(pairs[k][:, t // 2, :, :], turned[k][:, t - 1 : t + 1, :].rearrange("j e p -> j p e"))
+        staged = [sb("staged0", [P, PACK * HALF], BF16, tag="staging0"), sb("staged1", [P, PACK * P], BF16, tag="staging1")]
+        for k in range(blocks):
+            back = bank("back%d" % k, (3, 4, 5)[k], [P, 2, P])
+            words = pairs[k][:].rearrange("j u p e -> j (u p e)").bitcast(F32)
+            for u in range(2):
+                nc.tensor.transpose(back[:, u, :], words[:, u * P : (u + 1) * P], identity[:])
+            place = staged[k // 2][:].bitcast(F32)[:, 2 * P * (k % 2) : 2 * P * (k % 2 + 1)]
+            nc.scalar.copy(place.rearrange("p (j u) -> p j u", u=2), back[:].rearrange("p u j -> p j u"))
+        cand_s = deal(nc.vector, "cand_s", cand_s_list[:], U8, tag="b3")
+        cand_w = deal(nc.vector, "cand_w", cand_w_list[:].bitcast(I32), I32, tag="a3")
+        early = [bank("early%d" % t, (6, 7, 3, 4)[t], [P, EARLY]) for t in range(PACK)]
+        z_a = quantise("z_a", staged[0][:], HALF)
+        z_b = quantise("z_b", staged[1][:], P)
+        for t in range(PACK):
+            product(early[t][:, :HALF], cand_w, cand_s, t, z_a[0][:], z_a[1][:])
+            product(early[t][:, HALF:], cand_w, cand_s, t, z_b[0][:], z_b[1][:])
+        for t in range(PACK):
+            nc.scalar.activation(ex_win[t][:, :EARLY], early[t][:], ACT.Exp, scale=0.03125)
+            nc.sync.dma_start(ex_own[0][t][:], ex_win[t][:, :HALF])
+        for t in range(3):
+            nc.scalar.copy(s_win[t][:, :EARLY], early[t][:])
+
+        late_a = sb("late_a", [P, PACK, LATE], F32)
+        late_b = sb("late_b", [P, PACK, LATE], F32)
+        held = sb("held", [P, 2, 2, LATE], F32, tag="staging1")
+        for t in range(PACK):
+            diffs = held[:, t - 2, :, :] if t >= 2 else sb("late_diffs%d" % t, [P, 2, LATE], F32, tag="diffs", bufs=2)[:]
+            two_terms(t, EARLY, LATE, y_slim[t], y_wide[t], diffs, late_a[:, t, :], late_b[:, t, :])
+        staged_late = sb("staged_late", [P, PACK * LATE], BF16)
+        nc.vector.tensor_tensor(
+            staged_late[:].rearrange("p (c i t) -> p c t i", i=2, t=PACK),
+            late_a[:].rearrange("p t (c i) -> p c t i", i=2),
+            late_b[:].rearrange("p t (c i) -> p c t i", i=2),
+            ALU.add,
+        )
+        z_c = quantise("z_c", staged_late[:], LATE)
+        for t in range(3, PACK):
+            nc.vector.tensor_copy(s_win[t][:, :EARLY], early[t][:])
+        late = [bank("late%d" % t, (0, 1, 2, 5)[t], [P, LATE]) for t in range(PACK)]
+        for t in range(PACK):
+            product(late[t][:], cand_w, cand_s, t, z_c[0][:], z_c[1][:])
+        for t in range(PACK):
+            nc.scalar.activation(ex_win[t][:, EARLY:], late[t][:], ACT.Exp, scale=0.03125)
+            nc.sync.dma_start(ex_own[1][t][:], ex_win[t][:, HALF:])
+        for t in range(PACK):
+            nc.scalar.copy(s_win[t][:, EARLY:], late[t][:])
 
         ex5 = [[sb("ex5_%d_%d" % (h, t), [P, HALF], F32) for t in range(PACK)] for h in range(HALVES)]
         for h in range(HALVES):
             for t in range(PACK):
-                nc.scalar.activation(ex5[h][t][:], s_win[t][:].indirect(entries(n5_l, h)), ACT.Exp, scale=0.03125)
+                nc.scalar.activation(ex5[h][t][:], s_win[t][:].indirect(entries(n5_l, h * HALF, HALF)), ACT.Exp, scale=0.03125)
 
-        sums = [[sb("sums%d_%d" % (h, t), [P, 2, HALF], F32) for t in range(PACK)] for h in range(HALVES)]
+        sums = [sb("sums%d" % h, [P, PACK, 2, HALF], F32) for h in range(HALVES)]
         for h in range(HALVES):
             for t in range(PACK):
-                nc.vector.tensor_tensor(sums[h][t][:, 0, :], ex_win[t][:].indirect(entries(n4_l, h)), ex_own[h][t][:], ALU.add)
+                nc.vector.tensor_tensor(sums[h][:, t, 0, :], ex_win[t][:].indirect(entries(n4_l, h * HALF, HALF)), ex_own[h][t][:], ALU.add)
             for t in range(PACK):
-                nc.vector.tensor_tensor(sums[h][t][:, 1, :], ex_win[t][:].indirect(entries(n6_l, h)), ex5[h][t][:], ALU.add)
+                nc.vector.tensor_tensor(sums[h][:, t, 1, :], ex_win[t][:].indirect(entries(n6_l, h * HALF, HALF)), ex5[h][t][:], ALU.add)
 
         out_rows = out_0.rearrange("(p t) j -> p t j", t=PACK)
         out_words = out_1[0].rearrange("p n t -> p (n t)").bitcast(I32)
         o_s = sb("o_s", [P, S], U8)
-        for h in range(HALVES):
-            o = sb("o%d" % h, [P, PACK, HALF], F32)
-            for t in range(PACK):
-                logs = sb("logs%d_%d" % (h, t), [P, 2, HALF], F32)
-                nc.scalar.activation(logs[:], sums[h][t][:], ACT.Ln)
-                nc.vector.tensor_tensor(o[:, t, :], logs[:, 0, :], logs[:, 1, :], ALU.subtract)
-                nc.sync.dma_start(out_rows[:, t, cols(h)], o[:, t, :])
-            o_bf = sb("o_bf%d" % h, [P, PACK * HALF], BF16)
-            interleave(nc.vector.tensor_copy, o_bf, o)
-            o_w = sb("o_w%d" % h, [P, HALF], U32)
-            nc.vector.quantize_mx(out=o_w[:].bitcast(FP8X4), scales=o_s[:, cols(h)], in_=o_bf[:])
-            nc.sync.dma_start(out_words[:, cols(h)], o_w[:].bitcast(I32))
+        for n, (first, width, group) in enumerate(OUT_PIECES):
+            span = slice(first, first + width)
+            h = first // HALF
+            part = slice(first - h * HALF, first - h * HALF + width)
+            o = sb("o%d" % n, [P, PACK, width], F32)
+            logs = sb("logs%d" % n, [P, PACK, 2, width], F32)
+            for t in range(0, PACK, group):
+                tiles = slice(t, t + group)
+                nc.scalar.activation(logs[:, tiles, :, :], sums[h][:, tiles, :, part], ACT.Ln)
+                nc.vector.tensor_tensor(o[:, tiles, :], logs[:, tiles, 0, :], logs[:, tiles, 1, :], ALU.subtract)
+                nc.sync.dma_start(out_rows[:, tiles, span], o[:, tiles, :])
+            o_bf = sb("o_bf%d" % n, [P, PACK * width], BF16)
+            share = (96, 96)[n]
+            if share:
+                interleave(nc.scalar.copy, o_bf[:, : PACK * share], o[:, :, :share])
+            if share < width:
+                interleave(nc.vector.tensor_copy, o_bf[:, PACK * share :], o[:, :, share:])
+            o_w = sb("o_w%d" % n, [P, width], U32)
+            nc.vector.quantize_mx(out=o_w[:].bitcast(FP8X4), scales=o_s[:, span], in_=o_bf[:])
+            nc.sync.dma_start(out_words[:, span], o_w[:].bitcast(I32))
         for q in range(4):
             queue = nc.scalar if q % 2 == 0 else nc.sync
             queue.dma_start(out_2[0, 4 * q : 4 * q + 4, :].bitcast(I32), o_s[32 * q : 32 * q + 4, :].bitcast(I32))

from contextlib import ExitStack

import concourse.mybir as mybir
from concourse.masks import make_identity

K, T, S = 512, 2048, 512
FLOPS = 3 * 2 * 512 * 512 * 512

F32 = mybir.dt.float32
BF16 = mybir.dt.bfloat16
I32 = mybir.dt.int32
U32 = mybir.dt.uint32
U16 = mybir.dt.uint16
U8 = mybir.dt.uint8
FP8X4 = mybir.dt.float8_e4m3fn_x4
ACT = mybir.ActivationFunctionType
ALU = mybir.AluOpType

P = 128
PACK = 4
HALF = 256
HALVES = S // HALF
EARLY = 384
LATE = S - EARLY
WIDE = 2 * S
OUT_PIECES = ((0, 256, 4), (256, 256, 2))


def tile_picked_twcflowbodds_none_po_kernel(
    tc, x_words, x_scales, w1_words, w1_scales, w2_words, w2_scales, gs,
    offs, two, n1, n2, n3, cand, n4, n5, n6, out_0, out_1, out_2,
):
    nc = tc.nc
    with ExitStack() as ctx:
        lists = ctx.enter_context(tc.tile_pool(name="lists", bufs=1))
        keep = ctx.enter_context(tc.tile_pool(name="keep", bufs=1))
        psum = ctx.enter_context(tc.psum_pool(name="psum", bufs=1))

        def sb(name, shape, dtype, tag=None, bufs=1):
            return keep.tile(shape, dtype, name=name, tag=tag or name, bufs=bufs, align_bytes=64)

        def bank(name, number, shape):
            return psum.tile(shape, F32, name=name, tag="bank%d" % number)

        def load_list(name, source):
            tile = lists.tile([P, S // 16], U16, name=name)
            nc.sync.dma_start(tile[:], source)
            return tile

        def load_words(name, source, width):
            tile = sb(name, [P, width], I32)
            nc.sync.dma_start(tile[:], source[0].rearrange("p n t -> p (n t)").bitcast(I32))
            return tile

        def load_scales(tile, source, first, queues):
            for q in range(4):
                queues[q % len(queues)].dma_start(tile[32 * q + first : 32 * q + first + 4, :].bitcast(I32), source[0, 4 * q : 4 * q + 4, :].bitcast(I32))

        def deal(engine, name, source, dtype, tag=None):
            tile = sb(name, [P, S], dtype, tag=tag)
            run = 16 if dtype == U8 else 4
            engine.tensor_copy(
                tile[:].rearrange("p (t c i) -> p c t i", t=PACK, i=run),
                source.rearrange("p (c i t) -> p c t i", t=PACK, i=run),
            )
            return tile

        def entries(tile, first, width):
            return tile[:, first // 16 : (first + width) // 16]

        xs = sb("xs", [P, T], U8)
        ws_raw = sb("ws_raw", [P, S], U8)
        nc.vector.memset(xs[:].bitcast(I32), 0)
        nc.vector.memset(ws_raw[:].bitcast(I32), 0)

        w1w_raw = load_words("w1w_raw", w1_words, S)
        load_scales(xs, x_scales, 0, [nc.sync, nc.scalar])
        offs_l = load_list("offs_l", offs)
        two_l = load_list("two_l", two)
        xw = load_words("xw", x_words, T)
        load_scales(ws_raw, w1_scales, 0, [nc.sync])
        load_scales(ws_raw, w2_scales, 4, [nc.sync])
        w2w_raw = load_words("w2w_raw", w2_words, S)
        cand_l = load_list("cand_l", cand)
        gain = sb("gain", [P, PACK], F32)
        nc.sync.dma_start(gain[:], gs.rearrange("(p t) o -> p (t o)", t=PACK))
        n2_l = load_list("n2_l", n2)
        n1_l = load_list("n1_l", n1)
        n3_l = load_list("n3_l", n3)
        n4_l = load_list("n4_l", n4)
        n5_l = load_list("n5_l", n5)
        n6_l = load_list("n6_l", n6)

        half_gain = sb("half_gain", [P, PACK], F32)
        nc.scalar.activation(half_gain[:], gain[:], ACT.Copy, scale=0.5)

        def pick_bytes(name, offsets):
            tile = sb(name, [P, S], U8)
            nc.vector.tensor_copy(tile[:], xs[:].indirect(offsets[:]))
            return tile

        def pick_words(name, offsets):
            tile = sb(name, [P, S], U32)
            nc.vector.tensor_copy(tile[:], xw[:].bitcast(U32).indirect(offsets[:]))
            return tile

        w1w = deal(nc.vector, "w1w", w1w_raw[:], I32)
        offs_s = pick_bytes("offs_s", offs_l)
        two_s = pick_bytes("two_s", two_l)
        offs_w = pick_words("offs_w", offs_l)
        two_w = pick_words("two_w", two_l)
        ws = deal(nc.vector, "ws", ws_raw[:], U8)
        w2w = deal(nc.vector, "w2w", w2w_raw[:], I32)
        identity = sb("identity", [P, P], F32)
        make_identity(nc, identity[:])

        def product(result, lhs_w, lhs_s, t, rhs_w, rhs_s):
            rows = slice(t * P, (t + 1) * P)
            nc.tensor.matmul_mx(
                out=result, lhsT=lhs_w[:, rows].bitcast(FP8X4), lhsT_scale=lhs_s[:, rows],
                rhs=rhs_w.bitcast(FP8X4), rhs_scale=rhs_s, start=True, stop=True,
            )

        y_bank = [bank("y_bank%d" % t, t, [P, S]) for t in range(PACK)]
        d_bank = [bank("d_bank%d" % t, PACK + t, [P, S]) for t in range(PACK)]
        for t in range(PACK):
            product(y_bank[t][:], w1w, ws[:], t, offs_w[:], offs_s[:])
            product(d_bank[t][:], w2w, ws[4:P, :], t, two_w[:], two_s[:])

        y_wide = [sb("y_wide%d" % t, [P, WIDE], F32) for t in range(PACK)]
        y_slim = [sb("y_slim%d" % t, [P, S], F32) for t in range(PACK)]
        d_wide = [sb("d_wide%d" % t, [P, WIDE], F32) for t in range(PACK)]

        for t in range(PACK):
            nc.scalar.copy(y_wide[t][:, :S], y_bank[t][:])
            nc.scalar.copy(y_slim[t][:], y_bank[t][:])
            nc.scalar.activation(d_wide[t][:, :S], d_bank[t][:], ACT.Copy, scale=half_gain[:, t : t + 1])

        cand_s_list = pick_bytes("cand_s_list", cand_l)
        cand_w_list = pick_words("cand_w_list", cand_l)

        ex_win = [sb("ex_win%d" % t, [P, S], F32) for t in range(PACK)]
        s_win = [sb("s_win%d" % t, [P, S], F32) for t in range(PACK)]
        ex_own = [[sb("ex_own%d_%d" % (h, t), [P, HALF], F32) for t in range(PACK)] for h in range(HALVES)]

        def interleave(engine_copy, dst, src):
            engine_copy(dst.rearrange("p (c i t) -> p c t i", i=2, t=PACK), src.rearrange("p t (c i) -> p c t i", i=2))

        def two_terms(t, first, width, window, own, diffs, a, b):
            span = slice(first, first + width)
            nc.vector.tensor_tensor(diffs[:, 1, :], window[:].indirect(entries(n2_l, first, width)), own[:, span], ALU.subtract)
            nc.vector.tensor_tensor(diffs[:, 0, :], window[:].indirect(entries(n1_l, first, width)), own[:, span], ALU.subtract)
            nc.vector.tensor_tensor(b, d_wide[t][:].indirect(entries(n3_l, first, width)), diffs[:, 1, :], ALU.mult)
            nc.vector.scalar_tensor_tensor(a, d_wide[t][:, span], 2.0, diffs[:, 0, :], ALU.mult, ALU.mult)

        def quantise(name, staged, width):
            words = sb(name + "_w", [P, width], U32)
            scales = sb(name + "_s", [P, width], U8)
            nc.vector.quantize_mx(out=words[:].bitcast(FP8X4), scales=scales[:], in_=staged)
            return words, scales

        blocks = EARLY // P
        turned = [bank("turned%d" % k, k, [P, PACK, P]) for k in range(blocks)]
        pairs = [sb("pairs%d" % k, [P, 2, P, 2], BF16) for k in range(blocks)]
        for t in range(PACK):
            diffs = sb("diffs%d" % t, [P, 2, EARLY], F32, tag="diffs", bufs=2)
            a = sb("a%d" % t, [P, EARLY], F32)
            b = sb("b%d" % t, [P, EARLY], F32)
            two_terms(t, 0, EARLY, y_wide[t], y_slim[t], diffs, a[:], b[:])
            for k in range(blocks):
                part = slice(k * P, (k + 1) * P)
                nc.tensor.matmul(turned[k][:, t, :], b[:, part], identity[:], start=True, stop=False, is_transpose=True)
                nc.tensor.matmul(turned[k][:, t, :], a[:, part], identity[:], start=False, stop=True, is_transpose=True)
            if t % 2 == 1:
                for k in range(blocks):
                    nc.scalar.copy(pairs[k][:, t // 2, :, :], turned[k][:, t - 1 : t + 1, :].rearrange("j e p -> j p e"))
        staged = [sb("staged0", [P, PACK * HALF], BF16, tag="staging0"), sb("staged1", [P, PACK * P], BF16, tag="staging1")]
        for k in range(blocks):
            back = bank("back%d" % k, (3, 4, 5)[k], [P, 2, P])
            words = pairs[k][:].rearrange("j u p e -> j (u p e)").bitcast(F32)
            for u in range(2):
                nc.tensor.transpose(back[:, u, :], words[:, u * P : (u + 1) * P], identity[:])
            place = staged[k // 2][:].bitcast(F32)[:, 2 * P * (k % 2) : 2 * P * (k % 2 + 1)]
            nc.scalar.copy(place.rearrange("p (j u) -> p j u", u=2), back[:].rearrange("p u j -> p j u"))
        cand_s = deal(nc.vector, "cand_s", cand_s_list[:], U8, tag="b3")
        cand_w = deal(nc.vector, "cand_w", cand_w_list[:].bitcast(I32), I32, tag="a3")
        early = [bank("early%d" % t, (6, 7, 3, 4)[t], [P, EARLY]) for t in range(PACK)]
        z_a = quantise("z_a", staged[0][:], HALF)
        z_b = quantise("z_b", staged[1][:], P)
        for t in range(PACK):
            product(early[t][:, :HALF], cand_w, cand_s, t, z_a[0][:], z_a[1][:])
            product(early[t][:, HALF:], cand_w, cand_s, t, z_b[0][:], z_b[1][:])
        for t in range(PACK):
            nc.scalar.activation(ex_win[t][:, :EARLY], early[t][:], ACT.Exp, scale=0.03125)
            nc.sync.dma_start(ex_own[0][t][:], ex_win[t][:, :HALF])
        for t in range(3):
            nc.scalar.copy(s_win[t][:, :EARLY], early[t][:])

        late_a = sb("late_a", [P, PACK, LATE], F32)
        late_b = sb("late_b", [P, PACK, LATE], F32)
        held = sb("held", [P, 2, 2, LATE], F32, tag="staging1")
        for t in range(PACK):
            diffs = held[:, t - 2, :, :] if t >= 2 else sb("late_diffs%d" % t, [P, 2, LATE], F32, tag="diffs", bufs=2)[:]
            two_terms(t, EARLY, LATE, y_slim[t], y_wide[t], diffs, late_a[:, t, :], late_b[:, t, :])
        staged_late = sb("staged_late", [P, PACK * LATE], BF16)
        nc.vector.tensor_tensor(
            staged_late[:].rearrange("p (c i t) -> p c t i", i=2, t=PACK),
            late_a[:].rearrange("p t (c i) -> p c t i", i=2),
            late_b[:].rearrange("p t (c i) -> p c t i", i=2),
            ALU.add,
        )
        z_c = quantise("z_c", staged_late[:], LATE)
        for t in range(3, PACK):
            nc.vector.tensor_copy(s_win[t][:, :EARLY], early[t][:])
        late = [bank("late%d" % t, (0, 1, 2, 5)[t], [P, LATE]) for t in range(PACK)]
        for t in range(PACK):
            product(late[t][:], cand_w, cand_s, t, z_c[0][:], z_c[1][:])
        for t in range(PACK):
            nc.scalar.activation(ex_win[t][:, EARLY:], late[t][:], ACT.Exp, scale=0.03125)
            nc.sync.dma_start(ex_own[1][t][:], ex_win[t][:, HALF:])
        for t in range(PACK):
            nc.scalar.copy(s_win[t][:, EARLY:], late[t][:])

        ex5 = [[sb("ex5_%d_%d" % (h, t), [P, HALF], F32) for t in range(PACK)] for h in range(HALVES)]
        for h in range(HALVES):
            for t in range(PACK):
                nc.scalar.activation(ex5[h][t][:], s_win[t][:].indirect(entries(n5_l, h * HALF, HALF)), ACT.Exp, scale=0.03125)

        sums = [sb("sums%d" % h, [P, PACK, 2, HALF], F32) for h in range(HALVES)]
        for h in range(HALVES):
            for t in range(PACK):
                nc.vector.tensor_tensor(sums[h][:, t, 0, :], ex_win[t][:].indirect(entries(n4_l, h * HALF, HALF)), ex_own[h][t][:], ALU.add)
            for t in range(PACK):
                nc.vector.tensor_tensor(sums[h][:, t, 1, :], ex_win[t][:].indirect(entries(n6_l, h * HALF, HALF)), ex5[h][t][:], ALU.add)

        out_rows = out_0.rearrange("(p t) j -> p t j", t=PACK)
        out_words = out_1[0].rearrange("p n t -> p (n t)").bitcast(I32)
        o_s = sb("o_s", [P, S], U8)
        for n, (first, width, group) in enumerate(OUT_PIECES):
            span = slice(first, first + width)
            h = first // HALF
            part = slice(first - h * HALF, first - h * HALF + width)
            o = sb("o%d" % n, [P, PACK, width], F32)
            logs = sb("logs%d" % n, [P, PACK, 2, width], F32)
            for t in range(0, PACK, group):
                tiles = slice(t, t + group)
                nc.scalar.activation(logs[:, tiles, :, :], sums[h][:, tiles, :, part], ACT.Ln)
                nc.vector.tensor_tensor(o[:, tiles, :], logs[:, tiles, 0, :], logs[:, tiles, 1, :], ALU.subtract)
                nc.sync.dma_start(out_rows[:, tiles, span], o[:, tiles, :])
            o_bf = sb("o_bf%d" % n, [P, PACK * width], BF16)
            share = (96, 96)[n]
            if share:
                interleave(nc.scalar.copy, o_bf[:, : PACK * share], o[:, :, :share])
            if share < width:
                interleave(nc.vector.tensor_copy, o_bf[:, PACK * share :], o[:, :, share:])
            o_w = sb("o_w%d" % n, [P, width], U32)
            nc.vector.quantize_mx(out=o_w[:].bitcast(FP8X4), scales=o_s[:, span], in_=o_bf[:])
            nc.sync.dma_start(out_words[:, span], o_w[:].bitcast(I32))
        for q in range(4):
            queue = nc.scalar if q % 2 == 0 else nc.sync
            queue.dma_start(out_2[0, 4 * q : 4 * q + 4, :].bitcast(I32), o_s[32 * q : 32 * q + 4, :].bitcast(I32))
